import numpy as np
import ml_dtypes


def mxq(x, axis, fmt="e4m3"):
    dtype, down = {"e4m3": (ml_dtypes.float8_e4m3fn, 7), "e5m2": (ml_dtypes.float8_e5m2, 14)}[fmt]
    v = np.moveaxis(np.asarray(x, np.float32).astype(ml_dtypes.bfloat16).astype(np.float64), axis, -1)
    blocks = v.reshape(v.shape[:-1] + (-1, 32))
    amax = np.abs(blocks).max(-1, keepdims=True)
    byte = np.maximum(np.where(amax > 0, np.frexp(amax)[1] - 1 + 127, 0) - down, 1)
    scale = np.exp2(byte - 127.0)
    codes = (blocks / scale).astype(np.float32).astype(dtype).astype(np.float64)
    return np.moveaxis((codes * scale).reshape(v.shape), -1, axis)


WIDE = False


def mx_kscale(k):
    if not WIDE:
        return np.ones(k)
    levels = np.array([10, -10, 5, -5, 0])
    if k % 512:
        return np.exp2(np.random.permutation(np.resize(levels, k // 32))).repeat(32)
    a = np.empty((k // 512, 16))
    for p in range(k // 512):
        a[p, :8] = np.random.permutation(np.resize(levels, 8))
        for g in range(8):
            far = levels[np.abs(levels - a[p, g]) >= 10]
            a[p, g + 8] = far[np.random.randint(len(far))]
    return np.exp2(a.ravel()).repeat(32)


def f64(x):
    return np.asarray(x).astype(np.float64)


def striped(idx):
    return np.tile(idx.reshape(-1, 16).T, (8, 1)).astype(np.uint16)


def unstriped(offs):
    return offs[:16].T.reshape(-1).astype(np.int64)


def striped8(idx):
    return np.concatenate([x.reshape(-1, 16).T for x in idx]).astype(np.uint16)


def runs(offs, k):
    lists = np.stack([offs[16 * r : 16 * r + 16].T.reshape(-1) for r in range(8)]).astype(np.int64)
    return lists[np.arange(k) % 512 // 64]


def pack_weight(w):
    k, n = w.shape
    w = f64(np.asarray(w, np.float32).astype(ml_dtypes.bfloat16)).reshape(k // 32, 32, n)
    amax = np.abs(w).max(1)
    byte = np.clip(np.where(amax > 0, np.frexp(amax)[1] - 1 + 127 - 7, 1), 1, 254)
    scaled = (w * np.exp2(127.0 - byte)[:, None, :]).reshape(k, n).astype(np.float32)
    words = np.ascontiguousarray(scaled.reshape(k // 512, 128, 4, n).transpose(0, 1, 3, 2)).astype(ml_dtypes.float8_e4m3fn).view(np.uint8)
    return words, np.ascontiguousarray(byte.astype(np.uint8).reshape(k // 512, 16, n))


def unpack_weight(words, scales):
    g, p, n, _ = words.shape
    vals = np.ascontiguousarray(words).view(ml_dtypes.float8_e4m3fn).astype(np.float64) * np.repeat(np.exp2(scales.astype(np.float64) - 127.0), 8, axis=1)[..., None]
    return vals.transpose(0, 1, 3, 2).reshape(g * 512, n)

def planes(y):
    n, m = y.shape
    v = y.astype(np.float32).astype(ml_dtypes.bfloat16).astype(np.float64).reshape(n // 32, 32, m)
    top = np.abs(v).max(1)
    byte = np.clip(np.where(top > 0, np.frexp(top)[1] - 1 + 127 - 7, 1), 1, 254)
    codes = (v * np.exp2(127.0 - byte)[:, None, :]).reshape(n, m).astype(np.float32).astype(ml_dtypes.float8_e4m3fn).view(np.uint8)
    words = codes.reshape(n // 512, 128, 4, m).transpose(0, 1, 3, 2)
    return np.ascontiguousarray(words), np.ascontiguousarray(byte.astype(np.uint8).reshape(n // 512, 16, m))


K, T, S, G, H, W, C, U = 512, 1024, 512, 2048, 512, 256, 512, 1024


def setup_inputs():
    n = np.random.standard_normal
    s = mx_kscale(K)[:, None]
    packed_xT = pack_weight(n((K, T)) * s)
    packed_dT = pack_weight(n((K, G)) / s)
    perm = np.stack([np.random.permutation(S) for _ in range(8)])
    perm2 = np.stack([np.random.permutation(U) for _ in range(8)])
    return {
        "x_words": packed_xT[0],
        "x_scales": packed_xT[1],
        "d_words": packed_dT[0],
        "d_scales": packed_dT[1],
        "gs": (np.random.uniform(0.5, 1.5, (K, 1)) / s).astype(np.float32),
        "offs": striped8(np.random.randint(0, T, (8, S))),
        "k1": striped8(np.random.randint(0, G, (8, H))),
        "n1": striped8(perm[:, :W]),
        "n2": striped8(perm[:, W:]),
        "cand": striped(np.random.permutation(T)[:C]),
        "n3": striped8(perm2[:, :S]),
        "n4": striped8(perm2[:, S:]),
        "n5": striped8(np.stack([np.random.permutation(S) for _ in range(8)])),
    }


def reference(x_words, x_scales, d_words, d_scales, gs, offs, k1, n1, n2, cand, n3, n4, n5):
    x_cand = unpack_weight(x_words, x_scales)[:, unstriped(cand)]
    d_k1 = unpack_weight(d_words, d_scales)[np.arange(K)[:, None], runs(k1, K)]
    xq = unpack_weight(x_words, x_scales)[np.arange(K)[:, None], runs(offs, K)]
    h = 0.0625 * (d_k1.T @ xq)
    pa = h[np.arange(H)[:, None], runs(n1, H)]
    pb = h[np.arange(H)[:, None], runs(n2, H)]
    ra = np.maximum(pa, pb)
    ds = h.copy()
    ds[np.arange(H)[:, None], runs(n1, H)] = ra
    z = f64(gs) * ds
    s = 0.0625 * ((x_cand.T @ mxq(z, 0, "e4m3")))
    dn = np.minimum(s, s[np.arange(C)[:, None], runs(n5, C)])
    up = np.maximum(s, s[np.arange(C)[:, None], runs(n5, C)])
    ph = np.zeros((C, U))
    ph[np.arange(C)[:, None], runs(n3, C)] = up
    out = ph.copy()
    out[np.arange(C)[:, None], runs(n4, C)] = dn
    return (out,) + planes(out)

@@ -1,0 +1,194 @@
+from contextlib import ExitStack
+
+import concourse.mybir as mybir
+
+K, T, S, G, H, W, C, U = 512, 1024, 512, 2048, 512, 256, 512, 1024
+FLOPS = 2 * K * H * S + 2 * H * C * S
+
+F32 = mybir.dt.float32
+BF16 = mybir.dt.bfloat16
+I32 = mybir.dt.int32
+U32 = mybir.dt.uint32
+U16 = mybir.dt.uint16
+U8 = mybir.dt.uint8
+FP8X4 = mybir.dt.float8_e4m3fn_x4
+ALU = mybir.AluOpType
+COPY = mybir.ActivationFunctionType.Copy
+
+P = 128
+PACK = 4
+
+
+def tile_picked_hpqcfillpagmx_none_po_kernel(
+    tc, x_words, x_scales, d_words, d_scales, gs, offs, k1, n1, n2, cand, n3, n4, n5, out_0, out_1, out_2
+):
+    nc = tc.nc
+    with ExitStack() as ctx:
+        held = ctx.enter_context(tc.tile_pool(name="held", bufs=1))
+        psum = ctx.enter_context(tc.psum_pool(name="psum", bufs=1))
+
+        def load_list(name, dram):
+            tile = held.tile([P, dram.shape[1]], U16, name=name)
+            nc.sync.dma_start(tile[:], dram)
+            return tile
+
+        def dealt_view(ap):
+            return ap.rearrange("p (t m) -> p m t", t=PACK)
+
+        def listed_view(ap):
+            return ap.rearrange("p (m t) -> p m t", t=PACK)
+
+        xs_rows = x_scales[0].bitcast(I32)
+        ds_rows = d_scales[0].bitcast(I32)
+
+        xs_win = held.tile([P, T], U8, name="xs_win", align_bytes=64)
+        ds_win = held.tile([P, G], U8, name="ds_win", align_bytes=64)
+        placed = held.tile([P, S + H], U8, name="placed", align_bytes=64)
+        xc_sp = held.tile([P, C], U8, name="xc_sp", align_bytes=64)
+        nc.vector.memset(placed[:].bitcast(I32), 0)
+        nc.vector.memset(xc_sp[:].bitcast(I32), 0)
+
+        offs_t = load_list("offs_t", offs)
+        nc.sync.dma_start(xs_win[:].bitcast(I32), xs_rows.unsqueeze(1).broadcast_to([16, 8, T // 4]))
+        k1_t = load_list("k1_t", k1)
+        nc.sync.dma_start(ds_win[:].bitcast(I32), ds_rows.unsqueeze(1).broadcast_to([16, 8, G // 4]))
+        xw_win = held.tile([P, T], U32, name="xw_win", align_bytes=64)
+        dw_win = held.tile([P, G], U32, name="dw_win", align_bytes=64)
+        nc.sync.dma_start(xw_win[:].bitcast(I32), x_words[0].rearrange("p c r -> p (c r)").bitcast(I32))
+        nc.sync.dma_start(dw_win[:].bitcast(I32), d_words[0].rearrange("p c r -> p (c r)").bitcast(I32))
+        cand_t = load_list("cand_t", cand)
+        n1_t = load_list("n1_t", n1)
+        n2_t = load_list("n2_t", n2)
+        n5_t = load_list("n5_t", n5)
+        n3_t = load_list("n3_t", n3)
+        n4_t = load_list("n4_t", n4)
+        gs_t = held.tile([P, PACK], F32, name="gs_t")
+        nc.sync.dma_start(gs_t[:], gs.rearrange("(p t) o -> p (t o)", t=PACK))
+
+        xq_s = held.tile([P, S], U8, name="xq_s", align_bytes=64)
+        nc.vector.tensor_copy(xq_s[:], xs_win[:].indirect(offs_t[:]))
+        dk_s = held.tile([P, H], U8, name="dk_s", align_bytes=64)
+        nc.vector.tensor_copy(dk_s[:], ds_win[:].indirect(k1_t[:]))
+        staged = held.tile([P, S + H], U8, name="staged", align_bytes=64)
+        nc.vector.tensor_copy(dealt_view(staged[:, S : S + H]), listed_view(dk_s[:]))
+        nc.vector.tensor_copy(staged[:, 0:S].bitcast(I32), xq_s[:].bitcast(I32))
+        for i in range(4):
+            nc.scalar.dma_start(placed[:].bitcast(I32)[i:P:32, :], staged[:].bitcast(I32)[8 * i : P : 32, :])
+        xq_w = held.tile([P, S], U32, name="xq_w", align_bytes=64)
+        nc.vector.tensor_copy(xq_w[:], xw_win[:].indirect(offs_t[:]))
+        dk_w = held.tile([P, H], U32, name="dk_w", align_bytes=64)
+        nc.vector.tensor_copy(dk_w[:], dw_win[:].indirect(k1_t[:]))
+        dk_wd = held.tile([P, H], U32, name="dk_wd", align_bytes=64)
+        nc.vector.tensor_copy(dealt_view(dk_wd[:]), listed_view(dk_w[:]))
+
+        h_ps = []
+        for t in range(PACK):
+            acc = psum.tile([P, S], F32, name="h_ps%d" % t)
+            cols = slice(P * t, P * (t + 1))
+            nc.tensor.matmul_mx(
+                out=acc[:], lhsT=dk_wd[:, cols].bitcast(FP8X4), lhsT_scale=placed[:, S + P * t : S + P * (t + 1)],
+                rhs=xq_w[:].bitcast(FP8X4), rhs_scale=placed[:, 0:S], start=True, stop=True,
+            )
+            h_ps.append(acc)
+
+        xc_wd = held.tile([P, C], U32, name="xc_wd", align_bytes=64)
+        xc_sd = held.tile([P, C], U8, name="xc_sd", align_bytes=64)
+        nc.vector.tensor_copy(dealt_view(xc_wd[:]), xw_win[:].indirect(cand_t[:]))
+        nc.vector.tensor_copy(dealt_view(xc_sd[:]), xs_win[:].indirect(cand_t[:]))
+        for i in range(4):
+            nc.sync.dma_start(xc_sp[:].bitcast(I32)[i:P:32, :], xc_sd[:].bitcast(I32)[8 * i : P : 32, :])
+
+        ds = []
+        pairs = []
+        for t in range(PACK):
+            h = held.tile([P, S], F32, name="h%d" % t)
+            nc.scalar.activation(out=h[:], in_=h_ps[t][:], func=COPY, scale=0.0625)
+            pa = held.tile([P, W], F32, name="pa%d" % t)
+            pb = held.tile([P, W], F32, name="pb%d" % t)
+            nc.scalar.activation(out=pa[:], in_=h[:].indirect(n1_t[:]), func=COPY)
+            nc.scalar.activation(out=pb[:], in_=h[:].indirect(n2_t[:]), func=COPY)
+            ds.append(h)
+            pairs.append((pa, pb))
+
+        half = S // 2
+        halves = [slice(0, half), slice(half, S)]
+        z_bf = [held.tile([P, half, PACK], BF16, name="z_bf%d" % a, align_bytes=64) for a in range(2)]
+        for t in range(PACK):
+            pa, pb = pairs[t]
+            ra = held.tile([P, W], F32, name="ra%d" % t)
+            nc.vector.tensor_tensor(ra[:], pa[:], pb[:], ALU.max)
+            nc.vector.tensor_copy(ds[t][:].indirect(n1_t[:]), ra[:])
+            for a in range(2):
+                if t < 2:
+                    nc.scalar.activation(out=z_bf[a][:, :, t], in_=ds[t][:, halves[a]], func=COPY, scale=gs_t[:, t : t + 1])
+                else:
+                    nc.vector.tensor_scalar(z_bf[a][:, :, t], ds[t][:, halves[a]], gs_t[:, t : t + 1], None, ALU.mult)
+
+        z_w = held.tile([P, S], U32, name="z_w", align_bytes=64)
+        z_s = held.tile([P, S], U8, name="z_s", align_bytes=64)
+        for a in range(2):
+            nc.vector.quantize_mx(
+                out=z_w[:, halves[a]].bitcast(FP8X4), scales=z_s[:, halves[a]], in_=z_bf[a][:].rearrange("p c t -> p (c t)")
+            )
+
+        order = (2, 0, 1, 3)
+        s_sb = {}
+        mate = {}
+
+        def scores(acc, t, cols):
+            rows = slice(P * t, P * (t + 1))
+            nc.tensor.matmul_mx(
+                out=acc, lhsT=xc_wd[:, rows].bitcast(FP8X4), lhsT_scale=xc_sp[:, rows],
+                rhs=z_w[:, cols].bitcast(FP8X4), rhs_scale=z_s[:, cols], start=True, stop=True,
+            )
+
+        for t in order:
+            s_sb[t] = held.tile([P, S], F32, name="s%d" % t)
+            mate[t] = held.tile([P, S], F32, name="mate%d" % t)
+            lists = [n5_t[:, a * half // 16 : (a + 1) * half // 16] for a in range(2)]
+            if t == order[0]:
+                accs = [psum.tile([P, half], F32, name="s_first%d" % a, tag="h_ps%d" % a) for a in range(2)]
+                for a in range(2):
+                    scores(accs[a][:], t, halves[a])
+                nc.scalar.activation(out=s_sb[t][:, halves[0]], in_=accs[0][:], func=COPY, scale=0.0625)
+                nc.vector.tensor_scalar(s_sb[t][:, halves[1]], accs[1][:], 0.0625, None, ALU.mult)
+                nc.vector.tensor_copy(mate[t][:, halves[0]], s_sb[t][:].indirect(lists[0]))
+                nc.scalar.activation(out=mate[t][:, halves[1]], in_=s_sb[t][:].indirect(lists[1]), func=COPY)
+            else:
+                acc = psum.tile([P, S], F32, name="s_ps%d" % t)
+                scores(acc[:], t, slice(0, S))
+                nc.scalar.activation(out=s_sb[t][:], in_=acc[:], func=COPY, scale=0.0625)
+                for a in range(2):
+                    nc.scalar.activation(out=mate[t][:, halves[a]], in_=s_sb[t][:].indirect(lists[a]), func=COPY)
+
+        o_bf = [held.tile([P, U // 2, PACK], BF16, name="o_bf%d" % a, align_bytes=64) for a in range(2)]
+        out_rows = out_0.rearrange("(p t) c -> t p c", t=PACK)
+        for t in order:
+            up = held.tile([P, S], F32, name="up%d" % t, tag="page%d" % order[0] if t == order[-1] else "up%d" % t)
+            dn = held.tile([P, S], F32, name="dn%d" % t)
+            page = held.tile([P, U], F32, name="page%d" % t, tag="page%d" % t)
+            nc.vector.tensor_tensor(up[:], s_sb[t][:], mate[t][:], ALU.max)
+            nc.vector.tensor_tensor(dn[:], s_sb[t][:], mate[t][:], ALU.min)
+            nc.vector.tensor_copy(page[:].indirect(n3_t[:]), up[:])
+            nc.vector.tensor_copy(page[:].indirect(n4_t[:]), dn[:])
+            nc.sync.dma_start(out_rows[t], page[:])
+            for a in range(2):
+                cols = slice(a * U // 2, (a + 1) * U // 2)
+                if t == order[-1] and a == 0:
+                    nc.vector.tensor_copy(o_bf[a][:, :, t], page[:, cols])
+                else:
+                    nc.scalar.activation(out=o_bf[a][:, :, t], in_=page[:, cols], func=COPY)
+
+        o_w = held.tile([P, U], U32, name="o_w", align_bytes=64)
+        o_s = held.tile([P, U], U8, name="o_s", align_bytes=64)
+        words_out = out_1[0].rearrange("p c r -> p (c r)").bitcast(I32)
+        for a in range(2):
+            cols = slice(a * U // 2, (a + 1) * U // 2)
+            nc.vector.quantize_mx(
+                out=o_w[:, cols].bitcast(FP8X4), scales=o_s[:, cols], in_=o_bf[a][:].rearrange("p c t -> p (c t)")
+            )
+            nc.sync.dma_start(words_out[:, cols], o_w[:, cols].bitcast(I32))
+        scales_out = out_2[0].bitcast(I32)
+        for q in range(4):
+            eng = nc.scalar if q % 2 else nc.sync
+            eng.dma_start(scales_out[4 * q : 4 * q + 4, :], o_s[:].bitcast(I32)[32 * q : 32 * q + 4, :])

@@ -41,7 +41,7 @@ def tile_picked_hpqcfillpagmx_none_po_kernel(
         xs_rows = x_scales[0].bitcast(I32)
         ds_rows = d_scales[0].bitcast(I32)
 
-        xs_win = held.tile([P, T], U8, name="xs_win", align_bytes=64)
+        xs_win = held.tile([P, T], U8, name="xs_win", tag="xs_win", align_bytes=64)
         ds_win = held.tile([P, G], U8, name="ds_win", align_bytes=64)
         placed = held.tile([P, S + H], U8, name="placed", align_bytes=64)
         xc_sp = held.tile([P, C], U8, name="xc_sp", align_bytes=64)
@@ -52,18 +52,18 @@ def tile_picked_hpqcfillpagmx_none_po_kernel(
         nc.sync.dma_start(xs_win[:].bitcast(I32), xs_rows.unsqueeze(1).broadcast_to([16, 8, T // 4]))
         k1_t = load_list("k1_t", k1)
         nc.sync.dma_start(ds_win[:].bitcast(I32), ds_rows.unsqueeze(1).broadcast_to([16, 8, G // 4]))
-        xw_win = held.tile([P, T], U32, name="xw_win", align_bytes=64)
-        dw_win = held.tile([P, G], U32, name="dw_win", align_bytes=64)
-        nc.sync.dma_start(xw_win[:].bitcast(I32), x_words[0].rearrange("p c r -> p (c r)").bitcast(I32))
-        nc.sync.dma_start(dw_win[:].bitcast(I32), d_words[0].rearrange("p c r -> p (c r)").bitcast(I32))
+        xw_win = held.tile([P, T], U32, name="xw_win", tag="xw_win", align_bytes=64)
+        dw_win = held.tile([P, G], U32, name="dw_win", tag="dw_win", align_bytes=64)
         cand_t = load_list("cand_t", cand)
         n1_t = load_list("n1_t", n1)
         n2_t = load_list("n2_t", n2)
+        nc.sync.dma_start(xw_win[:].bitcast(I32), x_words[0].rearrange("p c r -> p (c r)").bitcast(I32))
+        nc.sync.dma_start(dw_win[:].bitcast(I32), d_words[0].rearrange("p c r -> p (c r)").bitcast(I32))
         n5_t = load_list("n5_t", n5)
         n3_t = load_list("n3_t", n3)
         n4_t = load_list("n4_t", n4)
         gs_t = held.tile([P, PACK], F32, name="gs_t")
-        nc.sync.dma_start(gs_t[:], gs.rearrange("(p t) o -> p (t o)", t=PACK))
+        nc.gpsimd.dma_start(gs_t[:], gs.rearrange("(p t) o -> p (t o)", t=PACK))
 
         xq_s = held.tile([P, S], U8, name="xq_s", align_bytes=64)
         nc.vector.tensor_copy(xq_s[:], xs_win[:].indirect(offs_t[:]))
@@ -76,23 +76,30 @@ def tile_picked_hpqcfillpagmx_none_po_kernel(
             nc.scalar.dma_start(placed[:].bitcast(I32)[i:P:32, :], staged[:].bitcast(I32)[8 * i : P : 32, :])
         xq_w = held.tile([P, S], U32, name="xq_w", align_bytes=64)
         nc.vector.tensor_copy(xq_w[:], xw_win[:].indirect(offs_t[:]))
-        dk_w = held.tile([P, H], U32, name="dk_w", align_bytes=64)
+        dk_w = held.tile([P, H], U32, name="dk_w", tag="dk_w", align_bytes=64)
         nc.vector.tensor_copy(dk_w[:], dw_win[:].indirect(k1_t[:]))
         dk_wd = held.tile([P, H], U32, name="dk_wd", align_bytes=64)
         nc.vector.tensor_copy(dealt_view(dk_wd[:]), listed_view(dk_w[:]))
 
-        h_ps = []
-        for t in range(PACK):
-            acc = psum.tile([P, S], F32, name="h_ps%d" % t)
-            cols = slice(P * t, P * (t + 1))
-            nc.tensor.matmul_mx(
-                out=acc[:], lhsT=dk_wd[:, cols].bitcast(FP8X4), lhsT_scale=placed[:, S + P * t : S + P * (t + 1)],
-                rhs=xq_w[:].bitcast(FP8X4), rhs_scale=placed[:, 0:S], start=True, stop=True,
-            )
-            h_ps.append(acc)
+        half = S // 2
+        halves = [slice(0, half), slice(half, S)]
 
-        xc_wd = held.tile([P, C], U32, name="xc_wd", align_bytes=64)
-        xc_sd = held.tile([P, C], U8, name="xc_sd", align_bytes=64)
+        def hidden(acc, t, cols):
+            nc.tensor.matmul_mx(
+                out=acc, lhsT=dk_wd[:, P * t : P * (t + 1)].bitcast(FP8X4), lhsT_scale=placed[:, S + P * t : S + P * (t + 1)],
+                rhs=xq_w[:, cols].bitcast(FP8X4), rhs_scale=placed[:, cols], start=True, stop=True,
+            )
+
+        h_first = [psum.tile([P, half], F32, name="h_first%d" % a, tag="first%d" % a) for a in range(2)]
+        for a in range(2):
+            hidden(h_first[a][:], 0, halves[a])
+        h_ps = {}
+        for t in range(1, PACK):
+            h_ps[t] = psum.tile([P, S], F32, name="h_ps%d" % t)
+            hidden(h_ps[t][:], t, slice(0, S))
+
+        xc_wd = held.tile([P, C], U32, name="xc_wd", tag="dk_w", align_bytes=64)
+        xc_sd = held.tile([P, C], U8, name="xc_sd", tag="dw_win", align_bytes=64)
         nc.vector.tensor_copy(dealt_view(xc_wd[:]), xw_win[:].indirect(cand_t[:]))
         nc.vector.tensor_copy(dealt_view(xc_sd[:]), xs_win[:].indirect(cand_t[:]))
         for i in range(4):
@@ -102,27 +109,44 @@ def tile_picked_hpqcfillpagmx_none_po_kernel(
         pairs = []
         for t in range(PACK):
             h = held.tile([P, S], F32, name="h%d" % t)
-            nc.scalar.activation(out=h[:], in_=h_ps[t][:], func=COPY, scale=0.0625)
-            pa = held.tile([P, W], F32, name="pa%d" % t)
+            if t == 0:
+                for a in range(2):
+                    nc.scalar.activation(out=h[:, halves[a]], in_=h_first[a][:], func=COPY, scale=0.0625)
+            else:
+                nc.scalar.activation(out=h[:], in_=h_ps[t][:], func=COPY, scale=0.0625)
+            pa = held.tile([P, W], F32, name="pa%d" % t, tag="xs_win" if t == 0 else "pa%d" % t, align_bytes=64)
             pb = held.tile([P, W], F32, name="pb%d" % t)
-            nc.scalar.activation(out=pa[:], in_=h[:].indirect(n1_t[:]), func=COPY)
+            if t == 0:
+                nc.vector.tensor_copy(pa[:], h[:].indirect(n1_t[:]))
+            else:
+                nc.scalar.activation(out=pa[:], in_=h[:].indirect(n1_t[:]), func=COPY)
             nc.scalar.activation(out=pb[:], in_=h[:].indirect(n2_t[:]), func=COPY)
             ds.append(h)
             pairs.append((pa, pb))
 
-        half = S // 2
-        halves = [slice(0, half), slice(half, S)]
+        z_rows = held.tile([P, PACK, S], BF16, name="z_rows", align_bytes=64)
         z_bf = [held.tile([P, half, PACK], BF16, name="z_bf%d" % a, align_bytes=64) for a in range(2)]
+        split = 320
         for t in range(PACK):
             pa, pb = pairs[t]
-            ra = held.tile([P, W], F32, name="ra%d" % t)
+            ra = held.tile([P, W], F32, name="ra%d" % t, tag="xw_win" if t == 0 else "ra%d" % t, align_bytes=64)
             nc.vector.tensor_tensor(ra[:], pa[:], pb[:], ALU.max)
             nc.vector.tensor_copy(ds[t][:].indirect(n1_t[:]), ra[:])
-            for a in range(2):
-                if t < 2:
-                    nc.scalar.activation(out=z_bf[a][:, :, t], in_=ds[t][:, halves[a]], func=COPY, scale=gs_t[:, t : t + 1])
-                else:
-                    nc.vector.tensor_scalar(z_bf[a][:, :, t], ds[t][:, halves[a]], gs_t[:, t : t + 1], None, ALU.mult)
+            if t < PACK - 1:
+                nc.scalar.activation(out=z_rows[:, t, :], in_=ds[t][:], func=COPY, scale=gs_t[:, t : t + 1])
+            else:
+                nc.vector.tensor_scalar(z_rows[:, t, 0:split], ds[t][:, 0:split], gs_t[:, t : t + 1], None, ALU.mult)
+                nc.scalar.activation(out=z_rows[:, t, split:S], in_=ds[t][:, split:S], func=COPY, scale=gs_t[:, t : t + 1])
+
+        def woven(ap):
+            return ap.rearrange("p (c i) t -> p c t i", i=4)
+
+        def by_fours(ap):
+            return ap.rearrange("p t (c i) -> p c t i", i=4)
+
+        nc.vector.tensor_copy(woven(z_bf[0][:]), by_fours(z_rows[:, :, 0:half]))
+        nc.vector.tensor_copy(woven(z_bf[1][:, 0 : split - half, :]), by_fours(z_rows[:, :, half:split]))
+        nc.scalar.copy(woven(z_bf[1][:, split - half : half, :]), by_fours(z_rows[:, :, split:S]))
 
         z_w = held.tile([P, S], U32, name="z_w", align_bytes=64)
         z_s = held.tile([P, S], U8, name="z_s", align_bytes=64)
@@ -147,21 +171,24 @@ def tile_picked_hpqcfillpagmx_none_po_kernel(
             mate[t] = held.tile([P, S], F32, name="mate%d" % t)
             lists = [n5_t[:, a * half // 16 : (a + 1) * half // 16] for a in range(2)]
             if t == order[0]:
-                accs = [psum.tile([P, half], F32, name="s_first%d" % a, tag="h_ps%d" % a) for a in range(2)]
+                accs = [psum.tile([P, half], F32, name="s_first%d" % a, tag="first%d" % a) for a in range(2)]
                 for a in range(2):
                     scores(accs[a][:], t, halves[a])
-                nc.scalar.activation(out=s_sb[t][:, halves[0]], in_=accs[0][:], func=COPY, scale=0.0625)
-                nc.vector.tensor_scalar(s_sb[t][:, halves[1]], accs[1][:], 0.0625, None, ALU.mult)
+                nc.vector.tensor_scalar(s_sb[t][:, halves[0]], accs[0][:], 0.0625, None, ALU.mult)
+                nc.scalar.activation(out=s_sb[t][:, halves[1]], in_=accs[1][:], func=COPY, scale=0.0625)
                 nc.vector.tensor_copy(mate[t][:, halves[0]], s_sb[t][:].indirect(lists[0]))
                 nc.scalar.activation(out=mate[t][:, halves[1]], in_=s_sb[t][:].indirect(lists[1]), func=COPY)
             else:
-                acc = psum.tile([P, S], F32, name="s_ps%d" % t)
+                acc = psum.tile([P, S], F32, name="s_ps%d" % t, tag="first1")
                 scores(acc[:], t, slice(0, S))
                 nc.scalar.activation(out=s_sb[t][:], in_=acc[:], func=COPY, scale=0.0625)
                 for a in range(2):
                     nc.scalar.activation(out=mate[t][:, halves[a]], in_=s_sb[t][:].indirect(lists[a]), func=COPY)
 
-        o_bf = [held.tile([P, U // 2, PACK], BF16, name="o_bf%d" % a, align_bytes=64) for a in range(2)]
+        spans = [slice(0, 512), slice(512, 768), slice(768, U)]
+        o_bf = [
+            held.tile([P, cols.stop - cols.start, PACK], BF16, name="o_bf%d" % a, align_bytes=64) for a, cols in enumerate(spans)
+        ]
         out_rows = out_0.rearrange("(p t) c -> t p c", t=PACK)
         for t in order:
             up = held.tile([P, S], F32, name="up%d" % t, tag="page%d" % order[0] if t == order[-1] else "up%d" % t)
@@ -172,8 +199,7 @@ def tile_picked_hpqcfillpagmx_none_po_kernel(
             nc.vector.tensor_copy(page[:].indirect(n3_t[:]), up[:])
             nc.vector.tensor_copy(page[:].indirect(n4_t[:]), dn[:])
             nc.sync.dma_start(out_rows[t], page[:])
-            for a in range(2):
-                cols = slice(a * U // 2, (a + 1) * U // 2)
+            for a, cols in enumerate(spans):
                 if t == order[-1] and a == 0:
                     nc.vector.tensor_copy(o_bf[a][:, :, t], page[:, cols])
                 else:
@@ -182,13 +208,14 @@ def tile_picked_hpqcfillpagmx_none_po_kernel(
         o_w = held.tile([P, U], U32, name="o_w", align_bytes=64)
         o_s = held.tile([P, U], U8, name="o_s", align_bytes=64)
         words_out = out_1[0].rearrange("p c r -> p (c r)").bitcast(I32)
-        for a in range(2):
-            cols = slice(a * U // 2, (a + 1) * U // 2)
+        for a in (1, 0, 2):
+            cols = spans[a]
             nc.vector.quantize_mx(
                 out=o_w[:, cols].bitcast(FP8X4), scales=o_s[:, cols], in_=o_bf[a][:].rearrange("p c t -> p (c t)")
             )
+        for cols in (slice(0, 768), slice(768, U)):
             nc.sync.dma_start(words_out[:, cols], o_w[:, cols].bitcast(I32))
         scales_out = out_2[0].bitcast(I32)
         for q in range(4):
-            eng = nc.scalar if q % 2 else nc.sync
+            eng = nc.sync if q == 3 else nc.scalar
             eng.dma_start(scales_out[4 * q : 4 * q + 4, :], o_s[:].bitcast(I32)[32 * q : 32 * q + 4, :])

@@ -49,7 +49,7 @@ def tile_picked_hpqcfillpagmx_none_po_kernel(
         nc.vector.memset(xc_sp[:].bitcast(I32), 0)
 
         offs_t = load_list("offs_t", offs)
-        nc.sync.dma_start(xs_win[:].bitcast(I32), xs_rows.unsqueeze(1).broadcast_to([16, 8, T // 4]))
+        nc.scalar.dma_start(xs_win[:].bitcast(I32), xs_rows.unsqueeze(1).broadcast_to([16, 8, T // 4]))
         k1_t = load_list("k1_t", k1)
         nc.sync.dma_start(ds_win[:].bitcast(I32), ds_rows.unsqueeze(1).broadcast_to([16, 8, G // 4]))
         xw_win = held.tile([P, T], U32, name="xw_win", tag="xw_win", align_bytes=64)
@@ -130,12 +130,17 @@ def tile_picked_hpqcfillpagmx_none_po_kernel(
         for t in range(PACK):
             pa, pb = pairs[t]
             ra = held.tile([P, W], F32, name="ra%d" % t, tag="xw_win" if t == 0 else "ra%d" % t, align_bytes=64)
-            nc.vector.tensor_tensor(ra[:], pa[:], pb[:], ALU.max)
-            nc.vector.tensor_copy(ds[t][:].indirect(n1_t[:]), ra[:])
+            for a in range(2):
+                part = slice(a * W // 2, (a + 1) * W // 2)
+                nc.vector.tensor_tensor(ra[:, part], pa[:, part], pb[:, part], ALU.max)
+            for a in range(2):
+                part = slice(a * W // 2, (a + 1) * W // 2)
+                nc.vector.tensor_copy(ds[t][:].indirect(n1_t[:, part.start // 16 : part.stop // 16]), ra[:, part])
             if t < PACK - 1:
                 nc.scalar.activation(out=z_rows[:, t, :], in_=ds[t][:], func=COPY, scale=gs_t[:, t : t + 1])
             else:
-                nc.vector.tensor_scalar(z_rows[:, t, 0:split], ds[t][:, 0:split], gs_t[:, t : t + 1], None, ALU.mult)
+                nc.vector.tensor_scalar(z_rows[:, t, 0:half], ds[t][:, 0:half], gs_t[:, t : t + 1], None, ALU.mult)
+                nc.vector.tensor_scalar(z_rows[:, t, half:split], ds[t][:, half:split], gs_t[:, t : t + 1], None, ALU.mult)
                 nc.scalar.activation(out=z_rows[:, t, split:S], in_=ds[t][:, split:S], func=COPY, scale=gs_t[:, t : t + 1])
 
         def woven(ap):
@@ -213,7 +218,6 @@ def tile_picked_hpqcfillpagmx_none_po_kernel(
             nc.vector.quantize_mx(
                 out=o_w[:, cols].bitcast(FP8X4), scales=o_s[:, cols], in_=o_bf[a][:].rearrange("p c t -> p (c t)")
             )
-        for cols in (slice(0, 768), slice(768, U)):
             nc.sync.dma_start(words_out[:, cols], o_w[:, cols].bitcast(I32))
         scales_out = out_2[0].bitcast(I32)
         for q in range(4):

from contextlib import ExitStack

import concourse.mybir as mybir

K, T, S, G, H, W, C, U = 512, 1024, 512, 2048, 512, 256, 512, 1024
FLOPS = 2 * K * H * S + 2 * H * C * S

F32 = mybir.dt.float32
BF16 = mybir.dt.bfloat16
I32 = mybir.dt.int32
U32 = mybir.dt.uint32
U16 = mybir.dt.uint16
U8 = mybir.dt.uint8
FP8X4 = mybir.dt.float8_e4m3fn_x4
ALU = mybir.AluOpType
COPY = mybir.ActivationFunctionType.Copy

P = 128
PACK = 4


def tile_picked_hpqcfillpagmx_none_po_kernel(
    tc, x_words, x_scales, d_words, d_scales, gs, offs, k1, n1, n2, cand, n3, n4, n5, out_0, out_1, out_2
):
    nc = tc.nc
    with ExitStack() as ctx:
        held = ctx.enter_context(tc.tile_pool(name="held", bufs=1))
        psum = ctx.enter_context(tc.psum_pool(name="psum", bufs=1))

        def load_list(name, dram):
            tile = held.tile([P, dram.shape[1]], U16, name=name)
            nc.sync.dma_start(tile[:], dram)
            return tile

        def dealt_view(ap):
            return ap.rearrange("p (t m) -> p m t", t=PACK)

        def listed_view(ap):
            return ap.rearrange("p (m t) -> p m t", t=PACK)

        xs_rows = x_scales[0].bitcast(I32)
        ds_rows = d_scales[0].bitcast(I32)

        xs_win = held.tile([P, T], U8, name="xs_win", tag="xs_win", align_bytes=64)
        ds_win = held.tile([P, G], U8, name="ds_win", align_bytes=64)
        placed = held.tile([P, S + H], U8, name="placed", align_bytes=64)
        xc_sp = held.tile([P, C], U8, name="xc_sp", align_bytes=64)
        nc.vector.memset(placed[:].bitcast(I32), 0)
        nc.vector.memset(xc_sp[:].bitcast(I32), 0)

        offs_t = load_list("offs_t", offs)
        nc.scalar.dma_start(xs_win[:].bitcast(I32), xs_rows.unsqueeze(1).broadcast_to([16, 8, T // 4]))
        k1_t = load_list("k1_t", k1)
        nc.sync.dma_start(ds_win[:].bitcast(I32), ds_rows.unsqueeze(1).broadcast_to([16, 8, G // 4]))
        xw_win = held.tile([P, T], U32, name="xw_win", tag="xw_win", align_bytes=64)
        dw_win = held.tile([P, G], U32, name="dw_win", tag="dw_win", align_bytes=64)
        cand_t = load_list("cand_t", cand)
        n1_t = load_list("n1_t", n1)
        n2_t = load_list("n2_t", n2)
        nc.sync.dma_start(xw_win[:].bitcast(I32), x_words[0].rearrange("p c r -> p (c r)").bitcast(I32))
        nc.sync.dma_start(dw_win[:].bitcast(I32), d_words[0].rearrange("p c r -> p (c r)").bitcast(I32))
        n5_t = load_list("n5_t", n5)
        n3_t = load_list("n3_t", n3)
        n4_t = load_list("n4_t", n4)
        gs_t = held.tile([P, PACK], F32, name="gs_t")
        nc.gpsimd.dma_start(gs_t[:], gs.rearrange("(p t) o -> p (t o)", t=PACK))

        xq_s = held.tile([P, S], U8, name="xq_s", align_bytes=64)
        nc.vector.tensor_copy(xq_s[:], xs_win[:].indirect(offs_t[:]))
        dk_s = held.tile([P, H], U8, name="dk_s", align_bytes=64)
        nc.vector.tensor_copy(dk_s[:], ds_win[:].indirect(k1_t[:]))
        staged = held.tile([P, S + H], U8, name="staged", align_bytes=64)
        nc.vector.tensor_copy(dealt_view(staged[:, S : S + H]), listed_view(dk_s[:]))
        nc.vector.tensor_copy(staged[:, 0:S].bitcast(I32), xq_s[:].bitcast(I32))
        for i in range(4):
            nc.scalar.dma_start(placed[:].bitcast(I32)[i:P:32, :], staged[:].bitcast(I32)[8 * i : P : 32, :])
        xq_w = held.tile([P, S], U32, name="xq_w", align_bytes=64)
        nc.vector.tensor_copy(xq_w[:], xw_win[:].indirect(offs_t[:]))
        dk_w = held.tile([P, H], U32, name="dk_w", tag="dk_w", align_bytes=64)
        nc.vector.tensor_copy(dk_w[:], dw_win[:].indirect(k1_t[:]))
        dk_wd = held.tile([P, H], U32, name="dk_wd", align_bytes=64)
        nc.vector.tensor_copy(dealt_view(dk_wd[:]), listed_view(dk_w[:]))

        half = S // 2
        halves = [slice(0, half), slice(half, S)]

        def hidden(acc, t, cols):
            nc.tensor.matmul_mx(
                out=acc, lhsT=dk_wd[:, P * t : P * (t + 1)].bitcast(FP8X4), lhsT_scale=placed[:, S + P * t : S + P * (t + 1)],
                rhs=xq_w[:, cols].bitcast(FP8X4), rhs_scale=placed[:, cols], start=True, stop=True,
            )

        h_first = [psum.tile([P, half], F32, name="h_first%d" % a, tag="first%d" % a) for a in range(2)]
        for a in range(2):
            hidden(h_first[a][:], 0, halves[a])
        h_ps = {}
        for t in range(1, PACK):
            h_ps[t] = psum.tile([P, S], F32, name="h_ps%d" % t)
            hidden(h_ps[t][:], t, slice(0, S))

        xc_wd = held.tile([P, C], U32, name="xc_wd", tag="dk_w", align_bytes=64)
        xc_sd = held.tile([P, C], U8, name="xc_sd", tag="dw_win", align_bytes=64)
        nc.vector.tensor_copy(dealt_view(xc_wd[:]), xw_win[:].indirect(cand_t[:]))
        nc.vector.tensor_copy(dealt_view(xc_sd[:]), xs_win[:].indirect(cand_t[:]))
        for i in range(4):
            nc.sync.dma_start(xc_sp[:].bitcast(I32)[i:P:32, :], xc_sd[:].bitcast(I32)[8 * i : P : 32, :])

        ds = []
        pairs = []
        for t in range(PACK):
            h = held.tile([P, S], F32, name="h%d" % t)
            if t == 0:
                for a in range(2):
                    nc.scalar.activation(out=h[:, halves[a]], in_=h_first[a][:], func=COPY, scale=0.0625)
            else:
                nc.scalar.activation(out=h[:], in_=h_ps[t][:], func=COPY, scale=0.0625)
            pa = held.tile([P, W], F32, name="pa%d" % t, tag="xs_win" if t == 0 else "pa%d" % t, align_bytes=64)
            pb = held.tile([P, W], F32, name="pb%d" % t)
            if t == 0:
                nc.vector.tensor_copy(pa[:], h[:].indirect(n1_t[:]))
            else:
                nc.scalar.activation(out=pa[:], in_=h[:].indirect(n1_t[:]), func=COPY)
            nc.scalar.activation(out=pb[:], in_=h[:].indirect(n2_t[:]), func=COPY)
            ds.append(h)
            pairs.append((pa, pb))

        z_rows = held.tile([P, PACK, S], BF16, name="z_rows", align_bytes=64)
        z_bf = [held.tile([P, half, PACK], BF16, name="z_bf%d" % a, align_bytes=64) for a in range(2)]
        split = 320
        for t in range(PACK):
            pa, pb = pairs[t]
            ra = held.tile([P, W], F32, name="ra%d" % t, tag="xw_win" if t == 0 else "ra%d" % t, align_bytes=64)
            for a in range(2):
                part = slice(a * W // 2, (a + 1) * W // 2)
                nc.vector.tensor_tensor(ra[:, part], pa[:, part], pb[:, part], ALU.max)
            for a in range(2):
                part = slice(a * W // 2, (a + 1) * W // 2)
                nc.vector.tensor_copy(ds[t][:].indirect(n1_t[:, part.start // 16 : part.stop // 16]), ra[:, part])
            if t < PACK - 1:
                nc.scalar.activation(out=z_rows[:, t, :], in_=ds[t][:], func=COPY, scale=gs_t[:, t : t + 1])
            else:
                nc.vector.tensor_scalar(z_rows[:, t, 0:half], ds[t][:, 0:half], gs_t[:, t : t + 1], None, ALU.mult)
                nc.vector.tensor_scalar(z_rows[:, t, half:split], ds[t][:, half:split], gs_t[:, t : t + 1], None, ALU.mult)
                nc.scalar.activation(out=z_rows[:, t, split:S], in_=ds[t][:, split:S], func=COPY, scale=gs_t[:, t : t + 1])

        def woven(ap):
            return ap.rearrange("p (c i) t -> p c t i", i=4)

        def by_fours(ap):
            return ap.rearrange("p t (c i) -> p c t i", i=4)

        nc.vector.tensor_copy(woven(z_bf[0][:]), by_fours(z_rows[:, :, 0:half]))
        nc.vector.tensor_copy(woven(z_bf[1][:, 0 : split - half, :]), by_fours(z_rows[:, :, half:split]))
        nc.scalar.copy(woven(z_bf[1][:, split - half : half, :]), by_fours(z_rows[:, :, split:S]))

        z_w = held.tile([P, S], U32, name="z_w", align_bytes=64)
        z_s = held.tile([P, S], U8, name="z_s", align_bytes=64)
        for a in range(2):
            nc.vector.quantize_mx(
                out=z_w[:, halves[a]].bitcast(FP8X4), scales=z_s[:, halves[a]], in_=z_bf[a][:].rearrange("p c t -> p (c t)")
            )

        order = (2, 0, 1, 3)
        s_sb = {}
        mate = {}

        def scores(acc, t, cols):
            rows = slice(P * t, P * (t + 1))
            nc.tensor.matmul_mx(
                out=acc, lhsT=xc_wd[:, rows].bitcast(FP8X4), lhsT_scale=xc_sp[:, rows],
                rhs=z_w[:, cols].bitcast(FP8X4), rhs_scale=z_s[:, cols], start=True, stop=True,
            )

        for t in order:
            s_sb[t] = held.tile([P, S], F32, name="s%d" % t)
            mate[t] = held.tile([P, S], F32, name="mate%d" % t)
            lists = [n5_t[:, a * half // 16 : (a + 1) * half // 16] for a in range(2)]
            if t == order[0]:
                accs = [psum.tile([P, half], F32, name="s_first%d" % a, tag="first%d" % a) for a in range(2)]
                for a in range(2):
                    scores(accs[a][:], t, halves[a])
                nc.vector.tensor_scalar(s_sb[t][:, halves[0]], accs[0][:], 0.0625, None, ALU.mult)
                nc.scalar.activation(out=s_sb[t][:, halves[1]], in_=accs[1][:], func=COPY, scale=0.0625)
                nc.vector.tensor_copy(mate[t][:, halves[0]], s_sb[t][:].indirect(lists[0]))
                nc.scalar.activation(out=mate[t][:, halves[1]], in_=s_sb[t][:].indirect(lists[1]), func=COPY)
            else:
                acc = psum.tile([P, S], F32, name="s_ps%d" % t, tag="first1")
                scores(acc[:], t, slice(0, S))
                nc.scalar.activation(out=s_sb[t][:], in_=acc[:], func=COPY, scale=0.0625)
                for a in range(2):
                    nc.scalar.activation(out=mate[t][:, halves[a]], in_=s_sb[t][:].indirect(lists[a]), func=COPY)

        spans = [slice(0, 512), slice(512, 768), slice(768, U)]
        o_bf = [
            held.tile([P, cols.stop - cols.start, PACK], BF16, name="o_bf%d" % a, align_bytes=64) for a, cols in enumerate(spans)
        ]
        out_rows = out_0.rearrange("(p t) c -> t p c", t=PACK)
        for t in order:
            up = held.tile([P, S], F32, name="up%d" % t, tag="page%d" % order[0] if t == order[-1] else "up%d" % t)
            dn = held.tile([P, S], F32, name="dn%d" % t)
            page = held.tile([P, U], F32, name="page%d" % t, tag="page%d" % t)
            nc.vector.tensor_tensor(up[:], s_sb[t][:], mate[t][:], ALU.max)
            nc.vector.tensor_tensor(dn[:], s_sb[t][:], mate[t][:], ALU.min)
            nc.vector.tensor_copy(page[:].indirect(n3_t[:]), up[:])
            nc.vector.tensor_copy(page[:].indirect(n4_t[:]), dn[:])
            nc.sync.dma_start(out_rows[t], page[:])
            for a, cols in enumerate(spans):
                if t == order[-1] and a == 0:
                    nc.vector.tensor_copy(o_bf[a][:, :, t], page[:, cols])
                else:
                    nc.scalar.activation(out=o_bf[a][:, :, t], in_=page[:, cols], func=COPY)

        o_w = held.tile([P, U], U32, name="o_w", align_bytes=64)
        o_s = held.tile([P, U], U8, name="o_s", align_bytes=64)
        words_out = out_1[0].rearrange("p c r -> p (c r)").bitcast(I32)
        for a in (1, 0, 2):
            cols = spans[a]
            nc.vector.quantize_mx(
                out=o_w[:, cols].bitcast(FP8X4), scales=o_s[:, cols], in_=o_bf[a][:].rearrange("p c t -> p (c t)")
            )
            nc.sync.dma_start(words_out[:, cols], o_w[:, cols].bitcast(I32))
        scales_out = out_2[0].bitcast(I32)
        for q in range(4):
            eng = nc.sync if q == 3 else nc.scalar
            eng.dma_start(scales_out[4 * q : 4 * q + 4, :], o_s[:].bitcast(I32)[32 * q : 32 * q + 4, :])
